import numpy as np
import ml_dtypes


def mxq(x, axis, fmt="e4m3"):
    dtype, down = {"e4m3": (ml_dtypes.float8_e4m3fn, 7), "e5m2": (ml_dtypes.float8_e5m2, 14)}[fmt]
    v = np.moveaxis(np.asarray(x, np.float32).astype(ml_dtypes.bfloat16).astype(np.float64), axis, -1)
    blocks = v.reshape(v.shape[:-1] + (-1, 32))
    amax = np.abs(blocks).max(-1, keepdims=True)
    byte = np.maximum(np.where(amax > 0, np.frexp(amax)[1] - 1 + 127, 0) - down, 1)
    scale = np.exp2(byte - 127.0)
    codes = (blocks / scale).astype(np.float32).astype(dtype).astype(np.float64)
    return np.moveaxis((codes * scale).reshape(v.shape), -1, axis)


WIDE = False


def mx_kscale(k):
    if not WIDE:
        return np.ones(k)
    levels = np.array([10, -10, 5, -5, 0])
    if k % 512:
        return np.exp2(np.random.permutation(np.resize(levels, k // 32))).repeat(32)
    a = np.empty((k // 512, 16))
    for p in range(k // 512):
        a[p, :8] = np.random.permutation(np.resize(levels, 8))
        for g in range(8):
            far = levels[np.abs(levels - a[p, g]) >= 10]
            a[p, g + 8] = far[np.random.randint(len(far))]
    return np.exp2(a.ravel()).repeat(32)


def f64(x):
    return np.asarray(x).astype(np.float64)


def striped8(idx):
    return np.asarray(idx).reshape(8, -1, 16).transpose(0, 2, 1).reshape(128, -1).astype(np.uint16)


def unstriped8(offs):
    return offs.reshape(8, 16, -1).transpose(0, 2, 1).reshape(8, -1).astype(np.int64)


def pick8(x, idx, run):
    r = np.arange(len(x))
    return x[r[:, None], idx[r % (8 * run) // run]]


E2M1 = np.array([0.0, 0.5, 1.0, 1.5, 2.0, 3.0, 4.0, 6.0, -0.0, -0.5, -1.0, -1.5, -2.0, -3.0, -4.0, -6.0])


def pack_weight(w, fmt):
    k, n = w.shape
    w = f64(np.asarray(w, np.float32).astype(ml_dtypes.bfloat16)).reshape(k // 32, 32, n)
    amax = np.abs(w).max(1)
    if fmt == "e4m3":
        byte = np.frexp(amax)[1] - 1 + 127 - 7
    else:
        mant, ex = np.frexp(amax / 6.0)
        byte = np.where(mant > 0.5, ex, ex - 1) + 127
    byte = np.clip(np.where(amax > 0, byte, 1), 1, 254)
    scaled = (w * np.exp2(127.0 - byte)[:, None, :]).reshape(k, n).astype(np.float32)
    by_word = np.ascontiguousarray(scaled.reshape(k // 512, 128, 4, n).transpose(0, 1, 3, 2))
    if fmt == "e4m3":
        words = by_word.astype(ml_dtypes.float8_e4m3fn).view(np.uint8)
    else:
        c = by_word.astype(ml_dtypes.float4_e2m1fn).view(np.uint8) & 0xF
        words = (c[..., 0::2] | (c[..., 1::2] << 4)).reshape(k // 512, 128, 2 * n)
    return np.ascontiguousarray(words), np.ascontiguousarray(byte.astype(np.uint8).reshape(k // 512, 16, n))


def unpack_weight(words, scales, fmt):
    g, _, n = scales.shape
    words = np.ascontiguousarray(words).reshape(g, 128, n, -1)
    if fmt == "e4m3":
        vals = words.view(ml_dtypes.float8_e4m3fn).astype(np.float64)
    else:
        nib = np.empty((g, 128, n, 4), np.uint8)
        nib[..., 0::2] = words & 0xF
        nib[..., 1::2] = words >> 4
        vals = E2M1[nib]
    vals = vals * np.repeat(np.exp2(scales.astype(np.float64) - 127.0), 8, axis=1)[..., None]
    return vals.transpose(0, 1, 3, 2).reshape(g * 512, n)


D, T, I, Q = 512, 1024, 512, 128


def setup_inputs():
    n = np.random.standard_normal
    idx = np.stack([np.random.permutation(T)[:I] for _ in range(8)])
    idx2 = np.stack([np.random.permutation(T)[:I] for _ in range(8)])
    idx3 = np.stack([np.random.permutation(T)[:I] for _ in range(8)])
    idx4 = np.stack([np.random.permutation(T)[:I] for _ in range(8)])
    idx5 = np.stack([np.random.permutation(T)[:I] for _ in range(8)])
    fd = mx_kscale(D)
    keysp = pack_weight(n((D, T)) / fd[:, None], "e4m3")
    tagsp = pack_weight(n((D, T)) / fd[:, None], "e2m1")
    return {
        "query": (n((D, Q)) * 0.75 / np.sqrt(D) * fd[:, None]).astype(np.float32),
        "query2": (n((D, Q)) * 0.75 / np.sqrt(D) * fd[:, None]).astype(np.float32),
        "keys_words": keysp[0],
        "keys_scales": keysp[1],
        "tags_words": tagsp[0],
        "tags_scales": tagsp[1],
        "offs": striped8(idx),
        "offs2": striped8(idx2),
        "offs3": striped8(idx3),
        "offs4": striped8(idx4),
        "offs5": striped8(idx5),
    }


def reference(query, query2, keys_words, keys_scales, tags_words, tags_scales, offs, offs2, offs3, offs4, offs5):
    idx = unstriped8(offs)
    idx2 = unstriped8(offs2)
    idx3 = unstriped8(offs3)
    idx4 = unstriped8(offs4)
    idx5 = unstriped8(offs5)
    keysu = unpack_weight(keys_words, keys_scales, "e4m3")
    tagsu = unpack_weight(tags_words, tags_scales, "e2m1")
    queryq = mxq(f64(query), 0, "e4m3")
    query2q = mxq(f64(query2), 0, "e4m3")
    a = queryq.T @ keysu + query2q.T @ tagsu
    ta = np.max(a, axis=1, keepdims=True)
    e1 = np.exp(pick8(a, idx, 16) - ta)
    f1 = np.zeros((Q, T))
    f1[np.arange(Q)[:, None], idx2[np.arange(Q) % 128 // 16]] = e1
    w = pick8(f1, idx3, 16) - e1
    f2 = np.zeros((Q, T))
    f2[np.arange(Q)[:, None], idx4[np.arange(Q) % 128 // 16]] = w
    cc = a + f2 * 4.0
    y = pick8(cc, idx5, 16)
    return y

@@ -1,0 +1,150 @@
+from contextlib import ExitStack
+
+import concourse.mybir as mybir
+
+D, T, I, Q = 512, 1024, 512, 128
+FLOPS = 2 * 2 * D * Q * T
+
+F32 = mybir.dt.float32
+BF16 = mybir.dt.bfloat16
+I32 = mybir.dt.int32
+U32 = mybir.dt.uint32
+U16 = mybir.dt.uint16
+U8 = mybir.dt.uint8
+FP8X4 = mybir.dt.float8_e4m3fn_x4
+FP4X4 = mybir.dt.float4_e2m1fn_x4
+ALU = mybir.AluOpType
+ACT = mybir.ActivationFunctionType
+
+P = 128
+PACK = 4
+HALF = I // 2
+PER_COL = 16
+PIECES = (256, 256, 256, 128, 128)
+
+
+def tile_attend_surplus_parts_kernel(
+    tc, query, query2, keys_words, keys_scales, tags_words, tags_scales,
+    offs, offs2, offs3, offs4, offs5, out,
+):
+    nc = tc.nc
+    with ExitStack() as ctx:
+        lists = ctx.enter_context(tc.tile_pool(name="lists", bufs=1))
+        keep = ctx.enter_context(tc.tile_pool(name="keep", bufs=1))
+        psum = ctx.enter_context(tc.psum_pool(name="psum", bufs=1))
+
+        tag_plane = keep.tile([P, T], U8, name="tag_plane", align_bytes=64)
+        key_plane = keep.tile([P, T], U8, name="key_plane", align_bytes=64)
+        nc.vector.memset(tag_plane[:].bitcast(I32), 0)
+        nc.vector.memset(key_plane[:].bitcast(I32), 0)
+
+        q2_raw = keep.tile([P, PACK, Q], F32, name="q2_raw")
+        q_raw = keep.tile([P, PACK, Q], F32, name="q_raw")
+        tag_words = keep.tile([P, 2 * T], U8, name="tag_words", align_bytes=64)
+        key_words = [keep.tile([P, T // 2], U32, name="key_words%d" % h, align_bytes=64) for h in range(2)]
+        keys_flat = keys_words[0].rearrange("p n t -> p (n t)").bitcast(I32)
+
+        def load_q2(e):
+            e.dma_start(out=q2_raw[:], in_=query2.rearrange("(p j) w -> p j w", j=PACK))
+
+        def load_q(e):
+            e.dma_start(out=q_raw[:], in_=query.rearrange("(p j) w -> p j w", j=PACK))
+
+        def load_tags(e):
+            e.dma_start(out=tag_words[:].bitcast(I32), in_=tags_words[0].bitcast(I32))
+
+        def load_keys(e, h):
+            e.dma_start(out=key_words[h][:].bitcast(I32), in_=keys_flat[:, h * 512 : (h + 1) * 512])
+
+        def load_plane(e, plane, scales, quad):
+            e.dma_start(
+                out=plane[32 * quad : 32 * quad + 4, :].bitcast(I32),
+                in_=scales[0, 4 * quad : 4 * quad + 4, :].bitcast(I32),
+            )
+
+        list_tiles = [lists.tile([P, I // PER_COL], U16, name="list%d" % n) for n in range(5)]
+
+        def load_lists():
+            for tile, src in zip(list_tiles, (offs, offs2, offs3, offs4, offs5)):
+                nc.sync.dma_start(tile[:], src)
+
+        load_q2(nc.sync)
+        load_q(nc.sync)
+        load_tags(nc.sync)
+        for quad in range(4):
+            load_plane(nc.scalar, tag_plane, tags_scales, quad)
+        for quad in range(4):
+            load_plane(nc.scalar, key_plane, keys_scales, quad)
+        load_keys(nc.sync, 0)
+        load_keys(nc.sync, 1)
+        load_lists()
+        idx, idx2, idx3, idx4, idx5 = list_tiles
+
+        f1 = keep.tile([P, T], F32, name="f1")
+        f2 = keep.tile([P, T], F32, name="f2")
+        nc.vector.memset(f1[:], 0.0)
+        nc.vector.memset(f2[:], 0.0)
+
+        q2_grp = keep.tile([P, Q, PACK], BF16, name="q2_grp", align_bytes=64)
+        q_grp = keep.tile([P, Q, PACK], BF16, name="q_grp", align_bytes=64)
+        nc.vector.tensor_copy(out=q2_grp[:], in_=q2_raw[:].rearrange("p j w -> p w j"))
+        nc.scalar.activation(out=q_grp[:], in_=q_raw[:].rearrange("p j w -> p w j"), func=ACT.Copy)
+        q2_codes = keep.tile([P, Q], U32, name="q2_codes", align_bytes=64)
+        q2_plane = keep.tile([P, Q], U8, name="q2_plane", align_bytes=64)
+        q_codes = keep.tile([P, Q], U32, name="q_codes", align_bytes=64)
+        q_plane = keep.tile([P, Q], U8, name="q_plane", align_bytes=64)
+        nc.vector.quantize_mx(out=q2_codes[:].bitcast(FP8X4), scales=q2_plane[:], in_=q2_grp[:].rearrange("p w j -> p (w j)"))
+        nc.vector.quantize_mx(out=q_codes[:].bitcast(FP8X4), scales=q_plane[:], in_=q_grp[:].rearrange("p w j -> p (w j)"))
+
+        a = keep.tile([P, T], F32, name="a")
+        piece_max = keep.tile([P, len(PIECES)], F32, name="piece_max")
+        start = 0
+        for n, width in enumerate(PIECES):
+            bank = psum.tile([P, width], F32, name="bank%d" % n)
+            h, within = divmod(start, T // 2)
+            nc.tensor.matmul_mx(
+                out=bank[:], lhsT=q2_codes[:].bitcast(FP8X4), lhsT_scale=q2_plane[:],
+                rhs=tag_words[:, 2 * start : 2 * (start + width)].bitcast(FP4X4),
+                rhs_scale=tag_plane[:, start : start + width], start=True, stop=False,
+            )
+            nc.tensor.matmul_mx(
+                out=bank[:], lhsT=q_codes[:].bitcast(FP8X4), lhsT_scale=q_plane[:],
+                rhs=key_words[h][:, within : within + width].bitcast(FP8X4),
+                rhs_scale=key_plane[:, start : start + width], start=False, stop=True,
+            )
+            nc.vector.tensor_scalar(
+                out=a[:, start : start + width], in0=bank[:], scalar1=1.0, scalar2=None,
+                op0=ALU.mult, op1=ALU.max, accum_out=piece_max[:, n : n + 1],
+            )
+            start += width
+        neg_ta = keep.tile([P, 1], F32, name="neg_ta")
+        nc.vector.tensor_reduce(out=neg_ta[:], in_=piece_max[:], axis=mybir.AxisListType.X, op=ALU.max, negate=True)
+
+        def slots(h):
+            return slice(h * HALF, (h + 1) * HALF)
+
+        def entries(h):
+            return slice(h * HALF // PER_COL, (h + 1) * HALF // PER_COL)
+
+        e1 = [keep.tile([P, HALF], F32, name="e1_%d" % h) for h in range(2)]
+        neg_e1 = [keep.tile([P, HALF], F32, name="neg_e1_%d" % h) for h in range(2)]
+        for h in range(2):
+            nc.scalar.activation(out=e1[h][:], in_=a[:].indirect(idx[:, entries(h)]), func=ACT.Exp, bias=neg_ta[:])
+        for h in range(2):
+            nc.vector.tensor_copy(out=f1[:].indirect(idx2[:, entries(h)]), in_=e1[h][:])
+            nc.scalar.activation(out=neg_e1[h][:], in_=e1[h][:], func=ACT.Copy, scale=-1.0)
+
+        found = [keep.tile([P, HALF], F32, name="found%d" % h) for h in range(2)]
+        nc.vector.tensor_copy(out=found[0][:], in_=f1[:].indirect(idx3[:, entries(0)]))
+        nc.scalar.activation(out=found[1][:], in_=f1[:].indirect(idx3[:, entries(1)]), func=ACT.Copy)
+        for h in range(2):
+            nc.vector.tensor_tensor(out=f2[:].indirect(idx4[:, entries(h)]), in0=found[h][:], in1=neg_e1[h][:], op=ALU.add)
+
+        cc = keep.tile([P, T], F32, name="cc")
+        nc.vector.scalar_tensor_tensor(out=cc[:], in0=f2[:], scalar=4.0, in1=a[:], op0=ALU.mult, op1=ALU.add)
+
+        y = [keep.tile([P, HALF], F32, name="y%d" % h) for h in range(2)]
+        nc.vector.tensor_copy(out=y[0][:], in_=cc[:].indirect(idx5[:, entries(0)]))
+        nc.scalar.activation(out=y[1][:], in_=cc[:].indirect(idx5[:, entries(1)]), func=ACT.Copy)
+        nc.sync.dma_start(out=out[:, slots(0)], in_=y[0][:])
+        nc.scalar.dma_start(out=out[:, slots(1)], in_=y[1][:])

@@ -20,7 +20,7 @@ P = 128
 PACK = 4
 HALF = I // 2
 PER_COL = 16
-PIECES = (256, 256, 256, 128, 128)
+PIECES = (256, 256, 256, 256)
 
 
 def tile_attend_surplus_parts_kernel(
@@ -69,13 +69,13 @@ def tile_attend_surplus_parts_kernel(
                 nc.sync.dma_start(tile[:], src)
 
         load_q2(nc.sync)
-        load_q(nc.sync)
+        for quad in range(4):
+            load_plane(nc.sync, tag_plane, tags_scales, quad)
         load_tags(nc.sync)
-        for quad in range(4):
-            load_plane(nc.scalar, tag_plane, tags_scales, quad)
-        for quad in range(4):
-            load_plane(nc.scalar, key_plane, keys_scales, quad)
+        load_q(nc.sync)
         load_keys(nc.sync, 0)
+        for quad in range(4):
+            load_plane(nc.sync, key_plane, keys_scales, quad)
         load_keys(nc.sync, 1)
         load_lists()
         idx, idx2, idx3, idx4, idx5 = list_tiles
@@ -87,8 +87,9 @@ def tile_attend_surplus_parts_kernel(
 
         q2_grp = keep.tile([P, Q, PACK], BF16, name="q2_grp", align_bytes=64)
         q_grp = keep.tile([P, Q, PACK], BF16, name="q_grp", align_bytes=64)
-        nc.vector.tensor_copy(out=q2_grp[:], in_=q2_raw[:].rearrange("p j w -> p w j"))
-        nc.scalar.activation(out=q_grp[:], in_=q_raw[:].rearrange("p j w -> p w j"), func=ACT.Copy)
+        for raw, grp in ((q2_raw, q2_grp), (q_raw, q_grp)):
+            nc.vector.tensor_copy(out=grp[:, :80, :], in_=raw[:, :, :80].rearrange("p j w -> p w j"))
+            nc.scalar.activation(out=grp[:, 80:, :], in_=raw[:, :, 80:].rearrange("p j w -> p w j"), func=ACT.Copy)
         q2_codes = keep.tile([P, Q], U32, name="q2_codes", align_bytes=64)
         q2_plane = keep.tile([P, Q], U8, name="q2_plane", align_bytes=64)
         q_codes = keep.tile([P, Q], U32, name="q_codes", align_bytes=64)
@@ -100,7 +101,7 @@ def tile_attend_surplus_parts_kernel(
         piece_max = keep.tile([P, len(PIECES)], F32, name="piece_max")
         start = 0
         for n, width in enumerate(PIECES):
-            bank = psum.tile([P, width], F32, name="bank%d" % n)
+            bank = psum.tile([P, width], F32, name="bank%d" % (n % 8), tag="bank%d" % (n % 8))
             h, within = divmod(start, T // 2)
             nc.tensor.matmul_mx(
                 out=bank[:], lhsT=q2_codes[:].bitcast(FP8X4), lhsT_scale=q2_plane[:],

@@ -41,7 +41,8 @@ def tile_attend_surplus_parts_kernel(
         q2_raw = keep.tile([P, PACK, Q], F32, name="q2_raw")
         q_raw = keep.tile([P, PACK, Q], F32, name="q_raw")
         tag_words = keep.tile([P, 2 * T], U8, name="tag_words", align_bytes=64)
-        key_words = [keep.tile([P, T // 2], U32, name="key_words%d" % h, align_bytes=64) for h in range(2)]
+        KCUT = (0, 768, T)
+        key_words = [keep.tile([P, KCUT[h + 1] - KCUT[h]], U32, name="key_words%d" % h, align_bytes=64) for h in range(2)]
         keys_flat = keys_words[0].rearrange("p n t -> p (n t)").bitcast(I32)
 
         def load_q2(e):
@@ -54,7 +55,7 @@ def tile_attend_surplus_parts_kernel(
             e.dma_start(out=tag_words[:].bitcast(I32), in_=tags_words[0].bitcast(I32))
 
         def load_keys(e, h):
-            e.dma_start(out=key_words[h][:].bitcast(I32), in_=keys_flat[:, h * 512 : (h + 1) * 512])
+            e.dma_start(out=key_words[h][:].bitcast(I32), in_=keys_flat[:, KCUT[h] : KCUT[h + 1]])
 
         def load_plane(e, plane, scales, quad):
             e.dma_start(
@@ -69,9 +70,10 @@ def tile_attend_surplus_parts_kernel(
                 nc.sync.dma_start(tile[:], src)
 
         load_q2(nc.sync)
-        for quad in range(4):
+        for quad in range(3):
             load_plane(nc.sync, tag_plane, tags_scales, quad)
         load_tags(nc.sync)
+        load_plane(nc.sync, tag_plane, tags_scales, 3)
         load_q(nc.sync)
         load_keys(nc.sync, 0)
         for quad in range(4):
@@ -102,7 +104,8 @@ def tile_attend_surplus_parts_kernel(
         start = 0
         for n, width in enumerate(PIECES):
             bank = psum.tile([P, width], F32, name="bank%d" % (n % 8), tag="bank%d" % (n % 8))
-            h, within = divmod(start, T // 2)
+            h = 0 if start < KCUT[1] else 1
+            within = start - KCUT[h]
             nc.tensor.matmul_mx(
                 out=bank[:], lhsT=q2_codes[:].bitcast(FP8X4), lhsT_scale=q2_plane[:],
                 rhs=tag_words[:, 2 * start : 2 * (start + width)].bitcast(FP4X4),
@@ -128,18 +131,17 @@ def tile_attend_surplus_parts_kernel(
             return slice(h * HALF // PER_COL, (h + 1) * HALF // PER_COL)
 
         e1 = [keep.tile([P, HALF], F32, name="e1_%d" % h) for h in range(2)]
-        neg_e1 = [keep.tile([P, HALF], F32, name="neg_e1_%d" % h) for h in range(2)]
+        neg_e1 = keep.tile([P, I], F32, name="neg_e1")
         for h in range(2):
             nc.scalar.activation(out=e1[h][:], in_=a[:].indirect(idx[:, entries(h)]), func=ACT.Exp, bias=neg_ta[:])
         for h in range(2):
             nc.vector.tensor_copy(out=f1[:].indirect(idx2[:, entries(h)]), in_=e1[h][:])
-            nc.scalar.activation(out=neg_e1[h][:], in_=e1[h][:], func=ACT.Copy, scale=-1.0)
+            nc.scalar.activation(out=neg_e1[:, slots(h)], in_=e1[h][:], func=ACT.Copy, scale=-1.0)
 
-        found = [keep.tile([P, HALF], F32, name="found%d" % h) for h in range(2)]
-        nc.vector.tensor_copy(out=found[0][:], in_=f1[:].indirect(idx3[:, entries(0)]))
-        nc.scalar.activation(out=found[1][:], in_=f1[:].indirect(idx3[:, entries(1)]), func=ACT.Copy)
-        for h in range(2):
-            nc.vector.tensor_tensor(out=f2[:].indirect(idx4[:, entries(h)]), in0=found[h][:], in1=neg_e1[h][:], op=ALU.add)
+        found = keep.tile([P, I], F32, name="found")
+        nc.vector.tensor_copy(out=found[:, slots(0)], in_=f1[:].indirect(idx3[:, entries(0)]))
+        nc.scalar.activation(out=found[:, slots(1)], in_=f1[:].indirect(idx3[:, entries(1)]), func=ACT.Copy)
+        nc.vector.tensor_tensor(out=f2[:].indirect(idx4[:]), in0=found[:], in1=neg_e1[:], op=ALU.add)
 
         cc = keep.tile([P, T], F32, name="cc")
         nc.vector.scalar_tensor_tensor(out=cc[:], in0=f2[:], scalar=4.0, in1=a[:], op0=ALU.mult, op1=ALU.add)

from contextlib import ExitStack

import concourse.mybir as mybir

D, T, I, Q = 512, 1024, 512, 128
FLOPS = 2 * 2 * D * Q * T

F32 = mybir.dt.float32
BF16 = mybir.dt.bfloat16
I32 = mybir.dt.int32
U32 = mybir.dt.uint32
U16 = mybir.dt.uint16
U8 = mybir.dt.uint8
FP8X4 = mybir.dt.float8_e4m3fn_x4
FP4X4 = mybir.dt.float4_e2m1fn_x4
ALU = mybir.AluOpType
ACT = mybir.ActivationFunctionType

P = 128
PACK = 4
HALF = I // 2
PER_COL = 16
PIECES = (256, 256, 256, 256)


def tile_attend_surplus_parts_kernel(
    tc, query, query2, keys_words, keys_scales, tags_words, tags_scales,
    offs, offs2, offs3, offs4, offs5, out,
):
    nc = tc.nc
    with ExitStack() as ctx:
        lists = ctx.enter_context(tc.tile_pool(name="lists", bufs=1))
        keep = ctx.enter_context(tc.tile_pool(name="keep", bufs=1))
        psum = ctx.enter_context(tc.psum_pool(name="psum", bufs=1))

        tag_plane = keep.tile([P, T], U8, name="tag_plane", align_bytes=64)
        key_plane = keep.tile([P, T], U8, name="key_plane", align_bytes=64)
        nc.vector.memset(tag_plane[:].bitcast(I32), 0)
        nc.vector.memset(key_plane[:].bitcast(I32), 0)

        q2_raw = keep.tile([P, PACK, Q], F32, name="q2_raw")
        q_raw = keep.tile([P, PACK, Q], F32, name="q_raw")
        tag_words = keep.tile([P, 2 * T], U8, name="tag_words", align_bytes=64)
        KCUT = (0, 768, T)
        key_words = [keep.tile([P, KCUT[h + 1] - KCUT[h]], U32, name="key_words%d" % h, align_bytes=64) for h in range(2)]
        keys_flat = keys_words[0].rearrange("p n t -> p (n t)").bitcast(I32)

        def load_q2(e):
            e.dma_start(out=q2_raw[:], in_=query2.rearrange("(p j) w -> p j w", j=PACK))

        def load_q(e):
            e.dma_start(out=q_raw[:], in_=query.rearrange("(p j) w -> p j w", j=PACK))

        def load_tags(e):
            e.dma_start(out=tag_words[:].bitcast(I32), in_=tags_words[0].bitcast(I32))

        def load_keys(e, h):
            e.dma_start(out=key_words[h][:].bitcast(I32), in_=keys_flat[:, KCUT[h] : KCUT[h + 1]])

        def load_plane(e, plane, scales, quad):
            e.dma_start(
                out=plane[32 * quad : 32 * quad + 4, :].bitcast(I32),
                in_=scales[0, 4 * quad : 4 * quad + 4, :].bitcast(I32),
            )

        list_tiles = [lists.tile([P, I // PER_COL], U16, name="list%d" % n) for n in range(5)]

        def load_lists():
            for tile, src in zip(list_tiles, (offs, offs2, offs3, offs4, offs5)):
                nc.sync.dma_start(tile[:], src)

        load_q2(nc.sync)
        for quad in range(3):
            load_plane(nc.sync, tag_plane, tags_scales, quad)
        load_tags(nc.sync)
        load_plane(nc.sync, tag_plane, tags_scales, 3)
        load_q(nc.sync)
        load_keys(nc.sync, 0)
        for quad in range(4):
            load_plane(nc.sync, key_plane, keys_scales, quad)
        load_keys(nc.sync, 1)
        load_lists()
        idx, idx2, idx3, idx4, idx5 = list_tiles

        f1 = keep.tile([P, T], F32, name="f1")
        f2 = keep.tile([P, T], F32, name="f2")
        nc.vector.memset(f1[:], 0.0)
        nc.vector.memset(f2[:], 0.0)

        q2_grp = keep.tile([P, Q, PACK], BF16, name="q2_grp", align_bytes=64)
        q_grp = keep.tile([P, Q, PACK], BF16, name="q_grp", align_bytes=64)
        for raw, grp in ((q2_raw, q2_grp), (q_raw, q_grp)):
            nc.vector.tensor_copy(out=grp[:, :80, :], in_=raw[:, :, :80].rearrange("p j w -> p w j"))
            nc.scalar.activation(out=grp[:, 80:, :], in_=raw[:, :, 80:].rearrange("p j w -> p w j"), func=ACT.Copy)
        q2_codes = keep.tile([P, Q], U32, name="q2_codes", align_bytes=64)
        q2_plane = keep.tile([P, Q], U8, name="q2_plane", align_bytes=64)
        q_codes = keep.tile([P, Q], U32, name="q_codes", align_bytes=64)
        q_plane = keep.tile([P, Q], U8, name="q_plane", align_bytes=64)
        nc.vector.quantize_mx(out=q2_codes[:].bitcast(FP8X4), scales=q2_plane[:], in_=q2_grp[:].rearrange("p w j -> p (w j)"))
        nc.vector.quantize_mx(out=q_codes[:].bitcast(FP8X4), scales=q_plane[:], in_=q_grp[:].rearrange("p w j -> p (w j)"))

        a = keep.tile([P, T], F32, name="a")
        piece_max = keep.tile([P, len(PIECES)], F32, name="piece_max")
        start = 0
        for n, width in enumerate(PIECES):
            bank = psum.tile([P, width], F32, name="bank%d" % (n % 8), tag="bank%d" % (n % 8))
            h = 0 if start < KCUT[1] else 1
            within = start - KCUT[h]
            nc.tensor.matmul_mx(
                out=bank[:], lhsT=q2_codes[:].bitcast(FP8X4), lhsT_scale=q2_plane[:],
                rhs=tag_words[:, 2 * start : 2 * (start + width)].bitcast(FP4X4),
                rhs_scale=tag_plane[:, start : start + width], start=True, stop=False,
            )
            nc.tensor.matmul_mx(
                out=bank[:], lhsT=q_codes[:].bitcast(FP8X4), lhsT_scale=q_plane[:],
                rhs=key_words[h][:, within : within + width].bitcast(FP8X4),
                rhs_scale=key_plane[:, start : start + width], start=False, stop=True,
            )
            nc.vector.tensor_scalar(
                out=a[:, start : start + width], in0=bank[:], scalar1=1.0, scalar2=None,
                op0=ALU.mult, op1=ALU.max, accum_out=piece_max[:, n : n + 1],
            )
            start += width
        neg_ta = keep.tile([P, 1], F32, name="neg_ta")
        nc.vector.tensor_reduce(out=neg_ta[:], in_=piece_max[:], axis=mybir.AxisListType.X, op=ALU.max, negate=True)

        def slots(h):
            return slice(h * HALF, (h + 1) * HALF)

        def entries(h):
            return slice(h * HALF // PER_COL, (h + 1) * HALF // PER_COL)

        e1 = [keep.tile([P, HALF], F32, name="e1_%d" % h) for h in range(2)]
        neg_e1 = keep.tile([P, I], F32, name="neg_e1")
        for h in range(2):
            nc.scalar.activation(out=e1[h][:], in_=a[:].indirect(idx[:, entries(h)]), func=ACT.Exp, bias=neg_ta[:])
        for h in range(2):
            nc.vector.tensor_copy(out=f1[:].indirect(idx2[:, entries(h)]), in_=e1[h][:])
            nc.scalar.activation(out=neg_e1[:, slots(h)], in_=e1[h][:], func=ACT.Copy, scale=-1.0)

        found = keep.tile([P, I], F32, name="found")
        nc.vector.tensor_copy(out=found[:, slots(0)], in_=f1[:].indirect(idx3[:, entries(0)]))
        nc.scalar.activation(out=found[:, slots(1)], in_=f1[:].indirect(idx3[:, entries(1)]), func=ACT.Copy)
        nc.vector.tensor_tensor(out=f2[:].indirect(idx4[:]), in0=found[:], in1=neg_e1[:], op=ALU.add)

        cc = keep.tile([P, T], F32, name="cc")
        nc.vector.scalar_tensor_tensor(out=cc[:], in0=f2[:], scalar=4.0, in1=a[:], op0=ALU.mult, op1=ALU.add)

        y = [keep.tile([P, HALF], F32, name="y%d" % h) for h in range(2)]
        nc.vector.tensor_copy(out=y[0][:], in_=cc[:].indirect(idx5[:, entries(0)]))
        nc.scalar.activation(out=y[1][:], in_=cc[:].indirect(idx5[:, entries(1)]), func=ACT.Copy)
        nc.sync.dma_start(out=out[:, slots(0)], in_=y[0][:])
        nc.scalar.dma_start(out=out[:, slots(1)], in_=y[1][:])
